import numpy as np, ml_dtypes
CORES = [9,25,41,57]
N = 4
BF = ml_dtypes.bfloat16
def gentries(a):
    return np.ascontiguousarray(a.reshape(8, 16, -1).transpose(0, 2, 1)).reshape(8, -1)
def gtable(e):
    e = np.asarray(e); return np.ascontiguousarray(e.reshape(8, -1, 16).transpose(0, 2, 1)).reshape(128, -1).astype(np.int32)
V, B, H, C, A, RO = 1024, 64, 16, 64, 3, 3
def names(rng, hub, *shape):
    g = np.arange(8).reshape((1, 8) + (1,) * (len(shape) - 2))
    return np.where(rng.random(shape) < 0.15, hub[g, rng.integers(0, 8, shape)], rng.integers(0, N * V, shape))
def place(rng, d, nm):
    return np.where(np.argsort(rng.random((N, 8, 16, V)), axis=2) < d[:, :, None, :], nm, N * V)
def plain(rng):
    hub = rng.integers(0, N * V, (8, 8))
    few = rng.choice(np.array([0.5, 1.0, 2.0, 3.0]), (N, 8, 1)) * H
    d = np.where(rng.random((N, 8, V)) < 0.03, 0, rng.integers(1, 13, (N, 8, V)))
    d = np.where(rng.random((N, 8, V)) * V < few, rng.integers(13, 17, (N, 8, V)), d)
    tall = rng.random((N, 8, 1, V)) * V < 0.5 * H
    x = (40000 * (0.7 + 0.3 * rng.random((N, 8, 1, V))) * rng.random((N, 8, 16, V))).astype(np.int64)
    x = np.where(tall, rng.integers(40000, 65536, (N, 8, 16, V)), x)
    a = rng.integers(0, V, (N, 8, RO * B)); b = names(rng, hub, N, 8, RO * B)
    return x, d, names(rng, hub, N, 8, 16, V), a, b, rng.integers(-2000, 2001, (N, 128, RO))
def pack(x, L, a, b, u):
    return {"x0": np.ascontiguousarray(x.reshape(N, 128, V)).astype(np.int32), "l0": np.ascontiguousarray(L.reshape(N, 128, V)).astype(np.int32),
            "ea": np.stack([gtable(k) for k in a]), "eb": np.stack([gtable(k) for k in b]), "u": np.ascontiguousarray(u).astype(np.int32)}
def tops(x, L):
    tab = np.concatenate([x[q] for q in range(N)] + [np.zeros((8, 16, 1), np.int64)], axis=2)
    m = np.zeros_like(x)
    for q in range(N):
        for i in range(16): m[q] = np.maximum(m[q], np.take_along_axis(tab, L[q, :, i][:, None, :], 2))
    return m, tab
def setup_inputs(rng):
    x, d, nm, a, b, u = plain(rng)
    return pack(x, place(rng, d, nm), a, b, u)
def setup_inputs_room(rng):
    x, d, nm, a, b, u = plain(rng); L = place(rng, np.minimum(d, 12), nm)
    x[:, 7, :, ::2] |= 2 ** 15; x[:, 7, :, 1::2] >>= 3; a[:, 7, :B] -= a[:, 7, :B] % 2
    for g in range(8): x[:, g, rng.permutation(16)[:5]] = 0
    for q in range(N):
        b[q, :, :B] = q * V + rng.integers(0, V, (8, B))
        e = (q + 1) % N; b[q, 7, :B] = e * V + 1 + 2 * rng.permutation(V // 2)[:B]
        for g in range(8):
            m = H + (0, 1, H)[int(rng.integers(0, 3))]
            if g == 1: m = H
            vs = np.sort(rng.permutation(V)[:m])
            if g == 1: vs[H - 1] = V - 1
            n = rng.choice(np.array([0, 1, C - 1, C, C + 1]), N)
            if g == 0: n[:] = C
            if g == 7: n[e] = max(C - B, 0)
            n[q] = 0; n[q] = 16 * H - int(np.sum(n))
            own = rng.permutation(np.repeat(np.arange(N), n))
            L[q, g][:, vs[:H]] = (own * V + rng.integers(0, V, 16 * H)).reshape(H, 16).T
            L[q, g][:, vs[H:]] = rng.integers(0, N * V, (16, m - H))
    return pack(x, L, a, b, u)
def setup_inputs_ties(rng):
    x, d, nm, a, b, u = plain(rng); h = V // 2
    base = rng.integers(0, 50000, (8, 16)); base[rng.integers(0, 8)] = rng.integers(61500, 65001, 16)
    base = np.broadcast_to(base[None, :, :, None], (N, 8, 16, h))
    x[..., :h] = np.take_along_axis(base, np.argsort(rng.random((N, 8, 16, h)), axis=2), 2)
    x[:, :, 0, :h] += rng.integers(0, 2, (N, 8, h))
    nm = (nm // V) * V + nm % h; low = d[..., :h]
    d[..., :h] = np.where(low > 12, 13, np.where(rng.random((N, 8, h)) < 0.5, 12, low)); d[..., h:] = rng.integers(1, 13, (N, 8, h))
    L = place(rng, d, nm); top = tops(x, L)[0][..., h:]
    share = rng.choice(np.array([1.0, 2.0, 6.0]), (N, 8, 1, 1)) * H
    rows = np.where(rng.random((N, 8, 1, h)) * V < share, rng.integers(12, 14, (N, 8, 1, h)), 11)
    x[..., h:] = np.where(np.argsort(rng.random((N, 8, 16, h)), axis=2) < rows, top + 1, top)
    m = rng.random(a.shape) < 0.5
    a = np.where(m, a % h, a); b = np.where(m, (b // V) * V + b % h, b)
    own = a + (np.arange(N) * V)[:, None, None]; z = N // 2 * 2
    b = np.where(rng.random(a.shape) < 0.1, own, b)
    b[0:z:2, :, ::8] = own[1:z:2, :, ::8]; b[1:z:2, :, ::8] = own[0:z:2, :, ::8]
    return pack(x, L, a, b, rng.integers(-1, 2, u.shape))
def setup_inputs_crowd(rng):
    x, d, nm, a, b, u = plain(rng); q = np.arange(N) * V
    ends = np.concatenate([q, q + V - 1, q + V // 2])
    nm = np.where(rng.random(nm.shape) < 0.5, rng.choice(ends, nm.shape), nm); b = np.where(rng.random(b.shape) < 0.5, rng.choice(ends, b.shape), b)
    nm = np.where(rng.random((N, 8, 1, V)) < 0.2, nm[:, :, :1], nm)
    nm = np.where(rng.random(nm.shape) < 0.05, q[:, None, None, None] + np.arange(V), nm)
    d = rng.choice(np.array([16, 15, 14, 13, 12, 10, 4]), (N, 8, V))
    d = np.where(np.arange(V) < rng.integers(0, V // 2, (N, 8, 1)), np.minimum(d, 12), d)
    d[:, :, 0] = np.array([16, 15, 14, 13, 12, 11, 14, 15]); d[:, :, V - 1] = np.array([13, 14, 16, 15, 11, 12, 16, 13]); d[:, :, V // 2] = rng.integers(11, 17, (N, 8))
    L = place(rng, d, nm)
    for g in (6, 7):
        o = int(rng.integers(0, N)); v = int(rng.integers(C // 16, V))
        b[:, g, :B] = o * V + v; L[:, g, :, :C // 16] = o * V + v
        x[o, g, :, v] = 0; L[o, g, rng.permutation(16)[:8], v] = N * V
    return pack(x, L, a, b, u)
def setup_inputs_quiet(rng):
    x, d, nm, a, b, u = plain(rng); g = rng.permutation(8); q = rng.permutation(N)
    d[q[0], g[2:]] = 16; d[q[1], g[2:]] = np.minimum(d[q[1], g[2:]], 12)
    d[:, g[0]] = 0; d[:, g[1]] = np.minimum(d[:, g[1]], 12); x[:, g[1], rng.permutation(16)[:5]] = 0
    d[q[2], g[1], V - 1] = 16
    z = rng.random(u.shape)
    u = np.where(z < 0.125, rng.choice(np.array([-65535, 65535]), u.shape), np.where(z < 0.375, rng.integers(-65535, 65536, u.shape), u))
    k = int(g[0]); x[:, k] = np.array(x[0, k, :, :1]); u[:, 16 * k:16 * k + 16] = np.array(u[0, 16 * k:16 * k + 16])
    return pack(x, place(rng, d, nm), a, b, u)
def setup_inputs_spread(rng):
    x, d, nm, a, b, u = plain(rng)
    x = np.minimum((np.exp2(16 * rng.random((N, 8, 1, V))) * rng.random((N, 8, 16, V))).astype(np.int64), 65535)
    d = (17 * rng.random((N, 8, V)) * rng.random((N, 8, V))).astype(np.int64)
    nm = (N * V * rng.random(nm.shape) * rng.random(nm.shape)).astype(np.int64)
    a = (V * rng.random(a.shape) * rng.random(a.shape)).astype(np.int64); b = (N * V * rng.random(b.shape) * rng.random(b.shape)).astype(np.int64)
    u = np.exp2(14 * rng.random(u.shape)).astype(np.int64) * rng.choice(np.array([-1, 1]), u.shape)
    return pack(x, place(rng, d, nm), a, b, u)
def check_inputs(d):
    bad = []
    for k, lo, hi in (("x0", 0, 65535), ("l0", 0, N * V), ("ea", 0, V - 1), ("eb", 0, N * V - 1), ("u", -65535, 65535)):
        if np.min(d[k]) < lo or np.max(d[k]) > hi: bad.append("range of " + k)
    return bad
def reference(x0, l0, ea, eb, u):
    none = N * V
    x = x0.astype(np.int64).reshape(N, 8, 16, V); L = l0.astype(np.int64).reshape(N, 8, 16, V); dr = u.astype(np.int64).reshape(N, 8, 16, RO)
    a = np.stack([gentries(k) for k in ea]).astype(np.int64); b = np.stack([gentries(k) for k in eb]).astype(np.int64)
    for t in range(RO):
        M, tab = tops(x, L); tot = np.add.reduce(tab, axis=1)
        deg = np.add.reduce((L < none).astype(np.int64), axis=2); votes = np.add.reduce((x > M).astype(np.int64), axis=2)
        inv = (deg > 12) | ((deg > 0) & (votes >= 12))
        inv = inv & (np.add.accumulate(inv.astype(np.int64), axis=2) <= H)
        new = np.array(L)
        for g in range(8):
            come = [[] for d in range(N)]
            for q in range(N):
                aa = a[q, g, t * B:(t + 1) * B] + q * V; bb = b[q, g, t * B:(t + 1) * B]; first = tot[g, aa] <= tot[g, bb]
                vs = np.nonzero(inv[q, g])[0]
                rec = np.concatenate([np.where(first, aa, bb), L[q, g][:, vs].T.reshape(-1)])
                giv = np.concatenate([np.where(first, bb, aa), np.repeat(vs + q * V, 16)])
                row = np.concatenate([np.full(B, -1), np.tile(np.arange(16), len(vs))])
                for d in range(N):
                    for s in np.nonzero((rec >= d * V) & (rec < (d + 1) * V))[0][:C]: come[d].append((int(rec[s]) - d * V, int(giv[s]), q, int(row[s])))
            for d in range(N):
                seen = {}
                for v, w, q, i in come[d]:
                    k = seen.get(v, 0); seen[v] = k + 1
                    if k >= A: continue
                    empty = np.nonzero(L[d, g, :, v] == none)[0]
                    if k < len(empty):
                        new[d, g, empty[k], v] = w
                        if i >= 0: new[q, g, i, w - q * V] = none
        x = np.clip(((x + M) >> 1) + dr[..., t:t + 1], 0, 65535); L = new
    return {"yx": x.reshape(N, 128, V).astype(np.float32), "yl": L.reshape(N, 128, V).astype(np.float32)}

from concourse.bass import DstId, RemoteDMATransfer
from concourse.mybir import AluOpType, AxisListType, ActivationFunctionType

N = 4
V = 1024
PV = V + 16
CH = 256
NCH = V // CH
SC = (0, 128, 240)
SL = (0, 128, 192, 240)
Q = V // 4
PATH = (0, 1, 2, 1)
REG = 320
RO = 3
F32, BF16, I32, U16 = "float32", "bfloat16", "int32", "uint16"

SCRATCH = {}


def _buf(kind, **sizes):
    for n in sizes:
        SCRATCH[n] = ("sbuf", [128, sizes[n]], kind)


_buf(I32, x0i=V, l0i=V, eai=12, ebi=12, ui=4, coli=128, gm=128, smi=128)
_buf(U16, ea16=12, eb16=12, xs=V, xu=N * V, lu=V, vn=2, off=20, vru=256, vw16=16, ok16=16, koff=2, exl=20)
_buf(F32, eaf=12, ebf=12, edab=12, uq=4, xt0=N * V + 8, xt1=N * V + 8, xt2=N * V + 8, L=PV, g0=16 * CH, g1=16 * CH,
     sc0=16 * CH, sc1=16 * CH, smf=1024, ex=320,
     w0=5 * REG, w1=5 * REG, w2=5 * REG, rq0=256, rq1=256, rq2=256, dd=3 * PV + 256, vws=256, tm=256,
     gr=256, val=256, cmpm=128, onf=128, ltm=128, i32=128, idf=128, iot=PV, j16=320, df=320)
_buf(BF16, emp=PV, f1=V, cmp=V, ripe=PV, cum=PV, cap=PV, sgo=CH + 16, ni=105, sp=105, ac0=5 * REG, ac1=5 * REG, ac2=5 * REG,
     as0=256, as1=256, as2=256, eg=256, eq=2176, mask=2176, ks=2176, ke=256, h=256, af=256, afs=256, onb=128, neg=128, oml=128,
     lm=128, i17=128, n17=128, rst=320, rs=2048)
for _k in range(8):
    SCRATCH["ps%d" % _k] = ("psum", [128, 512], F32)
WIDTH = {n: SCRATCH[n][1][1] for n in SCRATCH}
ALIAS = {"half": ("x0i", 0), "vri": ("x0i", CH)}
WIDTH["half"], WIDTH["vri"] = CH, 256


def _pieces(buf, **sizes):
    at = 0
    for n in sizes:
        ALIAS[n] = (buf, at)
        WIDTH[n] = sizes[n]
        at += (sizes[n] + 7) // 8 * 8


_pieces("smi", pidi=1, gpi=1, ri=1, exi=20, rec=20, own=20, cm=20)
_pieces("smf", sg=NCH, sgs=1, nli=16, giv=20, cf=20, cb=24, base=105, prod=105, pa=42, pb=21, pc=20, kx=16, b64=16, kk=16, tmv=16, t2=16,
        kc=16, o1=16, o2=16, o3=16, dl=16, nc=16, ga=64, gb=64, wd=64, wds=64, fw=4, ft=4, pid=1, gp=1, rr=1, rh=1, kt1=1, kt2=1, kt3=1,
        x16=16, xid=16, bias=2)

DSEM = ["ldx0", "ldx1", "ldl0", "ldl1", "ldea", "ldeb", "ldu"] + ["ox%d" % k for k in range(4)] + ["ol%d" % k for k in range(4)]
RSEM = ["ax%d" % k for k in range(4)] + ["hx"] + ["%s%d_%d" % (b, t, c) for b in ("bx", "hb") for t in (1, 2) for c in range(NCH)]
RSEM += ["%s%d" % (b, t) for b in ("rq", "ra") for t in range(RO)]
SEMAPHORES = ["v", "s", "p", "q", "loc"] + DSEM + RSEM

A = AluOpType
F = ActivationFunctionType


def rank_program(g, core, T, topo):
    rank = T.rank_of(core)

    def dst(c):
        ad = topo.addr(c)
        return DstId(rid=ad[0], pnc=ad[1])

    def emask(es):
        m = 0
        for e in es:
            m |= 1 << e
        return m

    def helpers(root):
        ok = [c for c in topo.cores_of(root) if c != root and all(topo.may_write(c, p) for p in T.cores if p != root)]
        return [c for c in ok if topo.die(c) == topo.die(root)][:1] + [c for c in ok if topo.die(c) != topo.die(root)][:2]

    if rank is None:
        roots = [r for r in T.cores if core in helpers(r)]
        if not roots:
            return
        root = roots[0]
        hn = helpers(root).index(core)
        peers = [c for c in T.cores if c != root]
        es = topo.engines(core, peers[0])
        own0 = T.rank_of(root) * V
        sent = [0]

        def forward(src, dap, rsem, asem, n):
            g.wait_ge(T.sem[asem], n)
            g.remote_dma_fused([RemoteDMATransfer(dst_ids=[dst(c) for c in peers], dma_engine_mask=emask(es), remote_sem=T.sem[rsem],
                                                  srcs=[src], dsts=[dap for c in peers], alu_op=0)], local_sem=T.sem.loc)
            sent[0] += len(es)

        lo = hn * Q
        forward(T.xs[:, lo:lo + Q], T.xu[:, own0 + lo:own0 + lo + Q], "ax%d" % hn, "hx", 4)
        near = [e for e in topo.engines(root, core) if e not in topo.engines(root, peers[0])]
        for t in (1, 2):
            for ch in range(NCH):
                if PATH[ch] == hn:
                    ap = T["xt%d" % t][:, own0 + ch * CH:own0 + ch * CH + CH]
                    forward(ap, ap, "bx%d_%d" % (t, ch), "hb%d_%d" % (t, ch), len(near))
        g.wait_ge(T.sem.loc, sent[0])
        return

    me = rank
    own0 = me * V
    peers = [c for c in T.cores if c != core]
    others = [r for r in range(N) if r != me]
    hs = helpers(core)
    far = topo.engines(core, peers[0])
    chip = topo.engines(core, hs[1])
    near = [e for e in chip if e not in far]
    eng = {"v": g.vector, "s": g.scalar, "p": g.tensor, "q": g, "y": g.sync}
    cnt = {"v": 0, "s": 0, "p": 0, "q": 0, "loc": 0}
    known = {k: {} for k in eng}
    snap = {}
    log = {n: [] for n in SCRATCH}
    events = {}

    def need(qn, evs):
        kn = known[qn]
        best = {}
        for s_, v_ in evs:
            if kn.get(s_, 0) < v_:
                best[s_] = max(best.get(s_, 0), v_)
        todo = list(best.items())
        for e in todo:
            if any(f is not e and snap.get(f, {}).get(e[0], 0) >= e[1] for f in todo):
                continue
            eng[qn].wait_ge(T.sem[e[0]], e[1])
        for e in todo:
            for s_, v_ in snap.get(e, {}).items():
                kn[s_] = max(kn.get(s_, 0), v_)
            kn[e[0]] = max(kn.get(e[0], 0), e[1])

    def deps(qn, reads, writes):
        evs = []
        for isw, regs in ((False, reads), (True, writes)):
            for (n, lo, hi) in regs:
                ps = n[:2] == "ps"
                for (l2, h2, w2, q2, ev) in log[n]:
                    over = l2 < hi and lo < h2
                    if q2 == qn:
                        hit = over and w2 and not (qn == "p" and isw)
                    else:
                        hit = ps or (over and (w2 or isw))
                    if hit:
                        evs.append(ev)
        return evs

    def record(qn, reads, writes, ev):
        for (n, lo, hi) in writes:
            log[n] = [x for x in log[n] if not (lo <= x[0] and x[1] <= hi)]
            log[n].append((lo, hi, True, qn, ev))
        for (n, lo, hi) in reads:
            log[n] = [x for x in log[n] if not ((not x[2]) and x[3] == qn and lo <= x[0] and x[1] <= hi)]
            log[n].append((lo, hi, False, qn, ev))

    def op(qn, reads, writes, fn):
        need(qn, deps(qn, reads, writes))
        ins = fn()
        cnt[qn] += 1
        ins.then_inc(T.sem[qn], 1)
        ev = (qn, cnt[qn])
        snap[ev] = dict(known[qn])
        record(qn, reads, writes, ev)

    def dma(qn, reads, writes, sem, out, in_):
        need(qn, deps(qn, reads, writes))
        eng[qn].dma_start(out, in_).then_inc(T.sem[sem], 16)
        events[sem] = 16
        snap[(sem, 16)] = dict(known[qn])
        record("dma_" + sem, reads, writes, (sem, 16))

    def arrive(regs, sem, total):
        events[sem] = total
        record("remote", [], regs, (sem, total))

    def a(n, lo=0, hi=None, st=1):
        hi = WIDTH[n] if hi is None else hi
        if n in ALIAS:
            n, at = ALIAS[n]
            lo, hi = at + lo, at + hi
        ap = T[n][:, lo:hi] if st == 1 else T[n][:, lo:hi:st]
        return (ap, (n, lo, hi), [])

    def ind(w, o):
        return (w[0].indirect(o[0]), w[1], [o[1]])

    def rd(*ops):
        r = []
        for o in ops:
            if isinstance(o, tuple):
                r.append(o[1])
                r.extend(o[2])
        return r

    def raw(o):
        return o[0] if isinstance(o, tuple) else o

    def cp(out, in_):
        op("v", rd(in_) + out[2], [out[1]], lambda: g.vector.tensor_copy(out[0], in_[0]))

    def tt(out, x, y, o):
        op("v", rd(x, y) + out[2], [out[1]], lambda: g.vector.tensor_tensor(out[0], x[0], y[0], o))

    def ts(out, x, s1, o0, s2=None, o1=None):
        if o1 is None:
            op("v", rd(x, s1), [out[1]], lambda: g.vector.tensor_scalar(out[0], x[0], raw(s1), None, o0))
        else:
            op("v", rd(x, s1, s2), [out[1]], lambda: g.vector.tensor_scalar(out[0], x[0], raw(s1), raw(s2), o0, o1))

    def ms(out, c):
        op("v", [], [out[1]], lambda: g.vector.memset(out[0], c))

    def scan(out, d0, d1, init, o0, o1):
        op("v", rd(d0, d1, init), [out[1]], lambda: g.vector.tensor_tensor_scan(out[0], d0[0], d1[0], raw(init), o0, o1))

    def act(out, in_, fn, bias=None, scale=None, accum=None):
        kw = {}
        if bias is not None:
            kw["bias"] = raw(bias)
        if scale is not None:
            kw["scale"] = scale
        if accum is not None:
            kw["accum_out"] = accum[0]
        op("s", rd(in_, bias), [out[1]] + ([accum[1]] if accum is not None else []), lambda: g.scalar.activation(out[0], in_[0], fn, **kw))

    def mm(out, lhsT, rhs, start, stop):
        op("p", rd(lhsT, rhs), [out[1]], lambda: g.tensor.matmul(out[0], lhsT[0], rhs[0], start, stop))

    def iota(out, pattern, base, cm):
        op("q", [], [out[1]], lambda: g.iota(out[0], pattern, base, cm, allow_small_or_imprecise_dtypes=True))

    def fused(trs, reads):
        need("q", deps("q", reads, []))
        g.remote_dma_fused([RemoteDMATransfer(dst_ids=[dst(c) for c in cs], dma_engine_mask=emask(es), remote_sem=T.sem[sem], srcs=[src],
                                              dsts=[dap for c in cs], alu_op=0) for cs, es, sem, src, dap in trs], local_sem=T.sem.loc)
        cnt["loc"] += sum(len(t[1]) for t in trs)

    def to_peers(parts, sem):
        per = 1
        while per * 2 * len(parts) <= len(far):
            per *= 2
        fused([([c], far[k * per:k * per + per], sem, src[0], dap) for k, (c, src, dap) in enumerate(parts)], [p[1][1] for p in parts])
        return per * (N - 1)

    H = V // 2
    dma("y", [], [("x0i", 0, H)], "ldx0", T.x0i[:, 0:H], T.x0[:, 0:H])
    dma("s", [], [("x0i", H, V)], "ldx1", T.x0i[:, H:V], T.x0[:, H:V])
    dma("y", [], [("l0i", 0, H)], "ldl0", T.l0i[:, 0:H], T.l0[:, 0:H])
    dma("s", [], [("l0i", H, V)], "ldl1", T.l0i[:, H:V], T.l0[:, H:V])
    dma("y", [], [("eai", 0, 12)], "ldea", T.eai[:, :], T.ea[:, :])
    dma("s", [], [("ebi", 0, 12)], "ldeb", T.ebi[:, :], T.eb[:, :])
    dma("y", [], [("ui", 0, 3)], "ldu", T.ui[:, 0:3], T.u[:, :])

    iota(a("pidi"), [[0, 1]], 0, 1)
    iota(a("coli"), [[1, 128]], 0, 0)
    iota(a("j16"), [[0, 20], [1, 16]], 0, 0)
    iota(a("exi"), [[1, 20]], 0, 0)

    ts(a("gpi"), a("pidi"), 4, A.arith_shift_right)
    ts(a("ri"), a("pidi"), 15, A.bitwise_and)
    ts(a("gm"), a("coli"), 4, A.arith_shift_right)
    cp(a("pid"), a("pidi"))
    cp(a("gp"), a("gpi"))
    cp(a("rr"), a("ri"))
    ts(a("onf"), a("gm"), a("gp"), A.is_equal)
    cp(a("onb"), a("onf"))
    ts(a("neg"), a("onf"), -1.0, A.mult)
    ts(a("n17"), a("onf"), -17.0, A.mult)
    ts(a("cmpm"), a("coli"), a("pid"), A.is_lt)
    ts(a("i32"), a("coli"), a("pid"), A.is_equal, -32.0, A.mult)
    ts(a("i17"), a("coli"), a("pid"), A.is_equal, 17.0, A.mult)
    ts(a("idf"), a("coli"), a("pid"), A.is_equal)
    tt(a("oml"), a("cmpm"), a("onf"), A.mult)

    for k in range(2):
        cp(a("xs", k * H, k * H + H), a("x0i", k * H, k * H + H))
    fused([([hs[k]], chip[j:j + 4], "hx", T.xs[:, k * Q:k * Q + Q], T.xs[:, k * Q:k * Q + Q]) for k, j in ((1, 8), (2, 12), (0, 4))], [("xs", 0, V)])
    fused([(peers, far, "ax3", T.xs[:, 3 * Q:V], T.xu[:, own0 + 3 * Q:own0 + V])], [("xs", 0, V)])
    for k in range(4):
        arrive([("xu", r * V + k * Q, r * V + k * Q + Q) for r in others], "ax%d" % k, len(far) * (N - 1))

    iota(a("g0", 0, 2048), [[0, 128], [1, 16]], 0, 0)
    iota(a("x16"), [[16, 16]], 0, 0)
    iota(a("iot"), [[1, PV]], own0, 0)
    iota(a("mask"), [[0, 2176]], 1, 0)
    iota(a("ac0"), [[0, 5 * REG]], 0, 0)
    iota(a("w0"), [[0, 5 * REG]], 262144, 0)
    iota(a("dd", 0, 3 * PV), [[0, 3 * PV]], 0, 0)

    for k in range(2):
        cp(a("lu", k * H, k * H + H), a("l0i", k * H, k * H + H))
        ts(a("emp", k * H, k * H + H), a("l0i", k * H, k * H + H), 4096.0, A.is_ge)
    cp(a("xt0", own0, own0 + V), a("x0i"))
    for t in range(RO):
        ms(a("xt%d" % t, N * V, N * V + 8), 0.0)
    ms(a("bias"), -4095.0)
    cp(a("L", 0, V), a("l0i"))
    ms(a("L", V, PV), 4096.0)
    ms(a("emp", V, PV), 1.0)
    ms(a("ripe", V, PV), 1.0)
    ms(a("cap"), 17.0)
    ms(a("ni"), 0.0)
    ms(a("base"), -1000.0)
    for d in range(5):
        ms(a("base", 21 * d, 21 * d + 1), 20.0 * (d + 1))
    ts(a("rh"), a("rr"), 0.5, A.add)
    cp(a("exl"), a("exi"))
    ts(a("df"), a("j16"), a("rr"), A.is_equal)
    ts(a("rst"), a("j16"), 0.5, A.is_ge)
    ts(a("cmpm"), a("coli"), a("pid"), A.is_gt)
    tt(a("ltm"), a("cmpm"), a("onf"), A.mult)
    tt(a("lm"), a("ltm"), a("i32"), A.add)
    cp(a("ea16"), a("eai"))
    cp(a("eb16"), a("ebi"))
    ts(a("eaf"), a("eai"), float(own0), A.add)
    cp(a("ebf"), a("ebi"))
    tt(a("edab"), a("eaf"), a("ebf"), A.subtract)
    ts(a("uq", 0, 3), a("ui", 0, 3), -0.25, A.add)
    cp(a("ps6", 0, 256), a("df", 0, 256))
    ts(a("kt1"), a("rr"), 1.0, A.add)
    ts(a("kt2"), a("rr"), -8.0, A.mult, 256.0, A.add)
    tt(a("kt3"), a("kt1"), a("kt2"), A.mult)
    for k in range(2):
        ts(a("koff", k, k + 1), a("kt3"), -1.0, A.add)
    ts(a("rs"), a("g0", 0, 2048), 0.5, A.is_lt, -65536.0, A.mult)

    def seg(c):
        return 256 * c - 8 * c * (c - 1)

    def degree():
        for k in range(2):
            mm(a("ps%d" % (1 + k), 0, 512), a("onb"), a("emp", k * 512, k * 512 + 512), True, True)

    def degree_flags():
        for k in range(2):
            ts(a("f1", k * 512, k * 512 + 512), a("ps%d" % (1 + k), 0, 512), 4.0, A.max, 15.0, A.min)

    degree()
    degree_flags()
    for k in (3, 0, 1, 2):
        for r in others:
            lo = r * V + k * Q
            cp(a("xt0", lo, lo + Q), a("xu", lo, lo + Q))

    def edges(t):
        xt = "xt%d" % t
        cp(a("ga"), ind(a(xt, own0, own0 + V), a("ea16", 4 * t, 4 * t + 4)))
        tt(a("gb"), ind(a(xt), a("eb16", 4 * t, 4 * t + 4)), a("ga"), A.subtract)
        mm(a("ps3", 0, 64), a("onf"), a("gb"), True, True)
        tt(a("wd"), a("ps3", 0, 64), a("df", 0, 64), A.mult)
        scan(a("wds"), a("rst", 0, 64), a("wd"), 0.0, A.mult, A.add)
        ts(a("fw"), a("wds", 15, 64, 16), 0.0, A.is_ge)
        tt(a("ft"), a("fw"), a("edab", 4 * t, 4 * t + 4), A.mult)
        tt(a("rec", 0, 4), a("ebf", 4 * t, 4 * t + 4), a("ft"), A.add)
        tt(a("giv", 0, 4), a("eaf", 4 * t, 4 * t + 4), a("ft"), A.subtract)

    def wcol(d):
        return REG * d + REG - 64, REG * d + REG

    def rcol(q):
        return (N - 1 - q) * 64, (N - 1 - q) * 64 + 64

    for t in range(RO):
        last = t == RO - 1
        xt, xn = "xt%d" % t, "xt%d" % (0 if last else t + 1)
        nown = 0 if last else own0

        def s_gather(ch):
            cuts = SL if ch == NCH - 1 else SC
            for lo, hi in zip(cuts[:-1], cuts[1:]):
                act(a("g%d" % (ch % 2), 16 * lo, 16 * hi), ind(a(xt), a("lu", ch * CH + lo, ch * CH + hi)), F.Copy)

        def newx(ch):
            lo, hi = ch * CH, (ch + 1) * CH
            ts(a("half"), a("ps0" if ch % 2 else "ps7", 0, CH), 0.5, A.mult, a("uq", t, t + 1), A.add)
            ts(a(xn, nown + lo, nown + hi), a("half"), 0.0, A.max, 65535.0, A.min)
            if last:
                dma("y", [(xn, lo, hi)], [], "ox%d" % ch, T.yx[:, lo:hi], T[xn][:, lo:hi])
            else:
                cols = (xn, own0 + lo, own0 + hi)
                ap = T[xn][:, own0 + lo:own0 + hi]
                fused([([hs[PATH[ch]]], near, "hb%d_%d" % (t + 1, ch), ap, ap)], [cols])
                arrive([(xn, r * V + lo, r * V + hi) for r in others], "bx%d_%d" % (t + 1, ch), len(far) * (N - 1))

        def ripe(ch):
            lo, hi = ch * CH, (ch + 1) * CH
            ts(a("ripe", lo, hi), a("ps%d" % (1 + ch % 2), 0, CH), 12.0, A.is_ge)
            he = PV if ch == NCH - 1 else hi
            scan(a("cum", lo, he), a("ripe", lo, he), a("cap", lo, he), a("cum", lo - 1, lo) if ch else 0.0, A.add, A.min)

        s_gather(0)
        if t > 0:
            act(a("emp", 0, V), a("L", 0, V), F.Relu, bias=a("bias", 0, 1))
        s_gather(1)
        for ch in range(NCH):
            gb, sb = "g%d" % (ch % 2), "sc%d" % (ch % 2)
            lo, hi = ch * CH, (ch + 1) * CH
            cuts = list(SL if ch == NCH - 1 else SC)
            cp(a(gb, 16 * cuts[-1], 16 * CH), ind(a(xt), a("lu", lo + cuts[-1], hi)))
            if ch == 0:
                edges(t)
                if t == 0:
                    ts(a("xid"), a("x16"), a("rr"), A.add, 1.0 / 64, A.mult)
                    for c in range(16):
                        ts(a("mask", seg(c), seg(c) + 16), a("j16", 0, 16), a("rr"), A.is_gt)
            cuts[-1] = CH
            for l2, h2 in zip(cuts[:-1], cuts[1:]):
                scan(a(sb, 16 * l2, 16 * h2), a("rs", 0, 16 * (h2 - l2)), a(gb, 16 * l2, 16 * h2), 0.0, A.add, A.max)
            if ch + 2 < NCH:
                s_gather(ch + 2)
            if ch == 0 and t > 0:
                degree()
                degree_flags()
            m = a(sb, 15, 16 * CH, 16)
            x = a(xt, own0 + lo, own0 + hi)
            tt(a("cmp", lo, hi), x, m, A.is_gt)
            vb = a("ps%d" % (1 + ch % 2), 0, CH)
            mm(vb, a("i17"), a("f1", lo, hi), True, False)
            mm(vb, a("n17"), a("emp", lo, hi), False, False)
            mm(vb, a("onb"), a("cmp", lo, hi), False, True)
            sm = a("ps0" if ch % 2 else "ps7", 0, CH)
            mm(sm, a("idf"), x, True, False)
            mm(sm, a("idf"), m, False, True)
            if ch > 0:
                newx(ch - 1)
                ripe(ch - 1)
        ripe(NCH - 1)
        for ch in range(NCH):
            lo, he = ch * CH, PV if ch == NCH - 1 else ch * CH + CH
            act(a("sgo", 0, he - lo), a("cum", lo, he), F.Sign, bias=a("rh"), scale=-1.0, accum=a("sg", ch, ch + 1))

        sga, sgb = a("sg"), a("sgs")
        op("v", [sga[1]], [sgb[1]], lambda: g.vector.tensor_reduce(sgb[0], sga[0], AxisListType.X, A.add))
        ts(a("vn", 0, 1), a("sgs"), 0.5, A.mult, PV / 2.0, A.add)
        vn = a("vn", 0, 1)
        cp(a("rec", 4, 20), ind(a("L"), vn))
        cp(a("giv", 4, 20), ind(a("iot"), vn))
        ts(a("own"), a("rec"), 10, A.arith_shift_right)
        ts(a("cm"), a("rec"), 1023, A.bitwise_and)
        for d in range(5):
            ts(a("ni", 21 * d + 1, 21 * d + 21), a("own"), float(d), A.is_equal, -1.0, A.mult)
        pp = a("ps3", 128, 233)
        mm(pp, a("oml"), a("ni"), True, False)
        scan(a("sp"), a("ni"), a("base"), 0.0, A.add, A.max)
        mm(pp, a("neg"), a("sp"), False, True)
        ts(a("cf"), a("cm"), 4096.0, A.mult)
        tt(a("cb", 0, 20), a("cf"), a("giv"), A.add)
        tt(a("ex"), ind(a("cb"), a("exl")), a("df"), A.mult)
        tt(a("prod"), a("ni"), pp, A.mult)
        tt(a("pa"), a("prod", 0, 42), a("prod", 42, 84), A.add)
        tt(a("pb"), a("pa", 0, 21), a("pa", 21, 42), A.add)
        tt(a("pc"), a("pb", 1, 21), a("prod", 85, 105), A.add)
        cp(a("off"), a("pc"))
        W, D, rqn, acn, asn = "w%d" % t, "dd", "rq%d" % t, "ac%d" % t, "as%d" % t
        cp(ind(a(W), a("off")), a("ex"))
        n = to_peers([(c, a(W, *wcol(T.rank_of(c))), T[rqn][:, rcol(me)[0]:rcol(me)[1]]) for c in peers], "rq%d" % t)
        arrive([(rqn,) + rcol(r) for r in others], "rq%d" % t, n)
        cp(a(rqn, *rcol(me)), a(W, *wcol(me)))
        newx(NCH - 1)
        ts(a("nli"), a("rec", 4, 20), -1.0, A.mult, 4096.0, A.add)
        if t > 0:
            iota(a(D, 0, 3 * PV), [[0, 3 * PV]], 0, 0)

        vr = a("ps4", 0, 256)
        mm(vr, a("onf"), a(rqn), True, True)
        ts(a("vri"), vr, 1.0 / 4096, A.mult, -0.4998779296875, A.add)
        tt(a("tm"), a("vri"), a("ps6", 0, 256), A.mult)
        cp(a("vru"), a("vri"))
        scan(a("vws"), a("rst", 0, 256), a("tm"), 0.0, A.mult, A.add)
        vw = a("vws", 15, 256, 16)
        cp(a("vw16"), vw)
        act(a("eg"), ind(a("emp"), a("vw16")), F.Copy)
        for c in range(16):
            ts(a("eq", seg(c), seg(c + 1)), a("vru", 16 * c, 256), a("vws", 16 * c + 15, 16 * c + 16), A.is_equal)
        dd = a("ps5", 0, 256)
        mm(dd, a("lm"), a("eg"), True, False)
        scan(a("ks"), a("eq"), a("mask"), 0.0, A.add, A.mult)
        ko = a("koff", 0, 1)
        cp(a("kx"), ind(a("ks"), ko))
        ts(a("b64"), ind(a("ks"), ko), 3.0, A.is_ge, 64.0, A.mult)
        tt(a("kk"), a("kx"), a("b64"), A.add)
        tt(a("ke"), ind(a("kk"), a("exl", 0, 16)), a("df", 0, 256), A.mult)
        mm(dd, a("neg"), a("ke"), False, True)
        ts(a("gr"), a("vri"), -4096.0, A.mult, -4096.0, A.add)
        ts(a("tmv"), vw, -1.0 / 64, A.mult)
        ts(a("h"), dd, -32.0, A.is_equal)
        mm(a("ps5", 256, 512), a("onb"), a("h"), True, True)
        act(a(asn), a("ps5", 256, 512), F.Copy)
        n = to_peers([(c, a(asn, *rcol(T.rank_of(c))), T[acn][:, wcol(me)[0]:wcol(me)[1]]) for c in peers], "ra%d" % t)
        arrive([(acn,) + wcol(r) for r in others], "ra%d" % t, n)
        act(a(acn, *wcol(me)), a("ps5", 256 + rcol(me)[0], 256 + rcol(me)[1]), F.Copy)
        if not last:
            iota(a("ac%d" % (t + 1)), [[0, 5 * REG]], 0, 0)
            iota(a("w%d" % (t + 1)), [[0, 5 * REG]], 262144, 0)
        ts(a("kc"), a("kx"), 3.0, A.min, float(PV), A.mult)
        tt(a("t2"), a("tmv"), a("xid"), A.add)
        tt(a("o1"), a("kc"), vw, A.add)
        tt(a("o2"), a("t2"), a("b64"), A.mult)
        tt(a("ps6", 256, 512), a("gr"), vr, A.add)
        tt(a("o3"), a("o1"), a("o2"), A.add)
        tt(a("val"), a("h"), a("ps6", 256, 512), A.mult)
        cp(a("ok16"), a("o3"))
        cp(ind(a(D), a("ok16")), a("val"))
        for j in range(3):
            for k, tp in ((0, a("ps0")), (1, a("ps7"))):
                lo, hi = k * 512, k * 512 + 512
                if j == 0:
                    tt(tp, a(D, lo, hi), a(D, PV + lo, PV + hi), A.add)
                elif j == 1:
                    tt(tp, a(D, 2 * PV + lo, 2 * PV + hi), tp, A.add)
                else:
                    tt(a("L", lo, hi), a("L", lo, hi), tp, A.add)

        tt(a("af"), ind(a(acn), a("off", 4, 20)), a("df", 0, 256), A.mult)
        scan(a("afs"), a("rst", 0, 256), a("af"), 0.0, A.mult, A.add)
        tt(a("dl"), a("afs", 15, 256, 16), a("nli"), A.mult)
        tt(a("nc"), ind(a("L"), vn), a("dl"), A.add)
        cp(ind(a("L"), vn), a("nc"))
        if last:
            for k in range(4):
                lo, hi = k * CH, k * CH + CH
                dma("ys"[k % 2], [("L", lo, hi)], [], "ol%d" % k, T.yl[:, lo:hi], T.L[:, lo:hi])
        else:
            for lo, hi in ((0, 128), (128, 256), (256, 1024)):
                cp(a("lu", lo, hi), a("L", lo, hi))

    for k in ("v", "s", "p", "q", "loc"):
        if known["q"].get(k, 0) < cnt[k]:
            g.wait_ge(T.sem[k], cnt[k])
    for s_, v_ in events.items():
        g.wait_ge(T.sem[s_], v_)
